import numpy as np
import ml_dtypes


def mxq(x, axis, fmt="e4m3"):
    dtype, down = {"e4m3": (ml_dtypes.float8_e4m3fn, 7), "e5m2": (ml_dtypes.float8_e5m2, 14)}[fmt]
    v = np.moveaxis(np.asarray(x, np.float32).astype(ml_dtypes.bfloat16).astype(np.float64), axis, -1)
    blocks = v.reshape(v.shape[:-1] + (-1, 32))
    amax = np.abs(blocks).max(-1, keepdims=True)
    byte = np.maximum(np.where(amax > 0, np.frexp(amax)[1] - 1 + 127, 0) - down, 1)
    scale = np.exp2(byte - 127.0)
    codes = (blocks / scale).astype(np.float32).astype(dtype).astype(np.float64)
    return np.moveaxis((codes * scale).reshape(v.shape), -1, axis)


WIDE = False


def mx_kscale(k):
    if not WIDE:
        return np.ones(k)
    levels = np.array([10, -10, 5, -5, 0])
    if k % 512:
        return np.exp2(np.random.permutation(np.resize(levels, k // 32))).repeat(32)
    a = np.empty((k // 512, 16))
    for p in range(k // 512):
        a[p, :8] = np.random.permutation(np.resize(levels, 8))
        for g in range(8):
            far = levels[np.abs(levels - a[p, g]) >= 10]
            a[p, g + 8] = far[np.random.randint(len(far))]
    return np.exp2(a.ravel()).repeat(32)


def f64(x):
    return np.asarray(x).astype(np.float64)


def striped(idx):
    return np.tile(idx.reshape(-1, 16).T, (8, 1)).astype(np.uint16)


def unstriped(offs):
    return offs[:16].T.reshape(-1).astype(np.int64)


E2M1 = np.array([0.0, 0.5, 1.0, 1.5, 2.0, 3.0, 4.0, 6.0, -0.0, -0.5, -1.0, -1.5, -2.0, -3.0, -4.0, -6.0])


def pack_weight(w, fmt):
    k, n = w.shape
    w = f64(np.asarray(w, np.float32).astype(ml_dtypes.bfloat16)).reshape(k // 32, 32, n)
    amax = np.abs(w).max(1)
    if fmt == "e4m3":
        byte = np.frexp(amax)[1] - 1 + 127 - 7
    else:
        mant, ex = np.frexp(amax / 6.0)
        byte = np.where(mant > 0.5, ex, ex - 1) + 127
    byte = np.clip(np.where(amax > 0, byte, 1), 1, 254)
    scaled = (w * np.exp2(127.0 - byte)[:, None, :]).reshape(k, n).astype(np.float32)
    by_word = np.ascontiguousarray(scaled.reshape(k // 512, 128, 4, n).transpose(0, 1, 3, 2))
    if fmt == "e4m3":
        words = by_word.astype(ml_dtypes.float8_e4m3fn).view(np.uint8)
    else:
        c = by_word.astype(ml_dtypes.float4_e2m1fn).view(np.uint8) & 0xF
        words = (c[..., 0::2] | (c[..., 1::2] << 4)).reshape(k // 512, 128, 2 * n)
    return np.ascontiguousarray(words), np.ascontiguousarray(byte.astype(np.uint8).reshape(k // 512, 16, n))


def unpack_weight(words, scales, fmt):
    g, _, n = scales.shape
    words = np.ascontiguousarray(words).reshape(g, 128, n, -1)
    if fmt == "e4m3":
        vals = words.view(ml_dtypes.float8_e4m3fn).astype(np.float64)
    else:
        nib = np.empty((g, 128, n, 4), np.uint8)
        nib[..., 0::2] = words & 0xF
        nib[..., 1::2] = words >> 4
        vals = E2M1[nib]
    vals = vals * np.repeat(np.exp2(scales.astype(np.float64) - 127.0), 8, axis=1)[..., None]
    return vals.transpose(0, 1, 3, 2).reshape(g * 512, n)


def gelu(v):
    return 0.5 * v * (1.0 + np.tanh(np.sqrt(2.0 / np.pi) * (v + 0.044715 * v**3)))


K, T, S, H, T2, P, N = 1536, 2048, 1024, 1024, 2048, 1024, 768

def setup_inputs():
    n = np.random.standard_normal
    s = mx_kscale(K)[:, None]
    u = mx_kscale(H)[:, None]
    tab_words, tab_scales = pack_weight(n((K, T)) * s, "e4m3")
    w1 = (n((K, H)) * 1.6 / np.sqrt(K) / s).astype(np.float32)
    b1 = (0.9 * n(H)).astype(np.float32)
    page0 = (n((H, T2)) * u).astype(np.float32)
    fc = (0.6 * n((H, P)) * u).astype(np.float32)
    w4_words, w4_scales = pack_weight(n((H, N)) / np.sqrt(H) / u, "e2m1")
    d = np.exp(0.4 * n(N)).astype(np.float32)
    offs = striped(np.random.permutation(T)[:S])
    offs2 = striped(np.random.permutation(T2)[:S])
    offs3 = striped(np.random.permutation(T2)[:P])
    return {"tab_words": tab_words, "tab_scales": tab_scales, "offs": offs,
            "offs2": offs2, "offs3": offs3, "w1": w1, "b1": b1,
            "page0": page0, "fc": fc, "w4_words": w4_words,
            "w4_scales": w4_scales, "d": d}

def reference(tab_words, tab_scales, offs, offs2, offs3, w1, b1, page0, fc, w4_words, w4_scales, d):
    v = unpack_weight(tab_words, tab_scales, "e4m3")[:, unstriped(offs)]
    h = np.tanh((mxq(f64(w1), 0, "e4m3").T @ v) + f64(b1)[:, None])
    page = f64(page0).copy()
    l2 = unstriped(offs2)
    page[:, l2] = page[:, l2] * (1.0 + 0.5 * h)
    x = page[:, unstriped(offs3)] + f64(fc)
    w4 = unpack_weight(w4_words, w4_scales, "e2m1")
    y = w4.T @ mxq(x, 0, "e4m3")
    return f64(d)[:, None] * y

@@ -1,0 +1,219 @@
+from contextlib import ExitStack
+
+import concourse.mybir as mybir
+
+K, T, S, H, T2, M, N = 1536, 2048, 1024, 1024, 2048, 1024, 768
+FLOPS = 2 * K * H * S + 2 * H * N * M
+
+F32 = mybir.dt.float32
+BF16 = mybir.dt.bfloat16
+I32 = mybir.dt.int32
+U32 = mybir.dt.uint32
+U16 = mybir.dt.uint16
+U8 = mybir.dt.uint8
+FP8X4 = mybir.dt.float8_e4m3fn_x4
+FP4X4 = mybir.dt.float4_e2m1fn_x4
+MULT = mybir.AluOpType.mult
+ADD = mybir.AluOpType.add
+COPY = mybir.ActivationFunctionType.Copy
+TANH = mybir.ActivationFunctionType.Tanh
+
+P = 128
+PACK = 4
+PASS = P * PACK
+BANK = 512
+K_PASSES = K // PASS
+R_PASSES = H // PASS
+N_TILES = N // P
+FC_WIDTH = 256
+CHUNKS = (256, 256, 256, 128, 128)
+
+
+def tile_list_heater_point_trust_kernel(
+    tc, tab_words, tab_scales, offs, offs2, offs3, w1, b1, page0, fc, w4_words, w4_scales, d, out
+):
+    nc = tc.nc
+    with ExitStack() as ctx:
+        keep = ctx.enter_context(tc.tile_pool(name="keep", bufs=1))
+        ring = ctx.enter_context(tc.tile_pool(name="ring", bufs=2))
+        psum = ctx.enter_context(tc.psum_pool(name="psum", bufs=8))
+
+        def stage(shape, dtype, name):
+            return ring.tile(shape, dtype, name=name, tag="stage", bufs=6)
+
+        idx = keep.tile([P, S // 16], U16, name="idx")
+        idx2 = keep.tile([P, S // 16], U16, name="idx2")
+        idx3 = keep.tile([P, M // 16], U16, name="idx3")
+        tab_planes = keep.tile([P, T], U8, name="tab_planes")
+        w4_planes = keep.tile([P, R_PASSES, N], U8, name="w4_planes", align_bytes=64)
+        w4_codes = keep.tile([P, R_PASSES, 2 * N], U8, name="w4_codes", align_bytes=64)
+        b1_cols = keep.tile([P, R_PASSES, PACK], F32, name="b1_cols")
+        d_cols = keep.tile([P, N_TILES], F32, name="d_cols")
+        v_planes = keep.tile([P, S], U8, name="v_planes", align_bytes=64)
+        v_codes = [keep.tile([P, S], U32, name="v_codes%d" % a, align_bytes=64) for a in range(K_PASSES)]
+        pages = [keep.tile([P, T2], F32, name="page%d" % i) for i in range(R_PASSES * PACK)]
+
+        nc.vector.memset(tab_planes[:].bitcast(I32), 0)
+        nc.vector.memset(w4_planes[:].rearrange("p a n -> p (a n)").bitcast(I32), 0)
+
+        nc.sync.dma_start(idx[:], offs)
+
+        def gather_table(a):
+            words = stage([P, T], I32, "words%d" % a)
+            nc.sync.dma_start(words[:], tab_words[a].rearrange("p n i -> p (n i)").bitcast(I32))
+            nc.vector.tensor_copy(v_codes[a][:], words[:].bitcast(U32).indirect(idx[:]))
+
+        w1_q = {}
+
+        def quantize_w1(a, b):
+            raw = stage([P, PACK, PASS], F32, "w1raw%d%d" % (a, b))
+            nc.sync.dma_start(
+                raw[:],
+                w1[PASS * a : PASS * (a + 1), PASS * b : PASS * (b + 1)].rearrange("(p j) c -> p j c", j=PACK),
+            )
+            for u in range(2):
+                rounded = ring.tile([P, 2 * PASS], BF16, name="w1bf", tag="w1bf", bufs=4, align_bytes=64)
+                nc.scalar.copy(
+                    rounded[:].rearrange("p (e m j) -> p m j e", e=2, j=PACK),
+                    raw[:].rearrange("p j (m u e) -> p u m j e", u=2, e=2)[:, u],
+                )
+                codes = keep.tile([P, 2 * P], U32, name="w1c%d%d%d" % (a, b, u), align_bytes=64)
+                plane = keep.tile([P, 2 * P], U8, name="w1s%d%d%d" % (a, b, u), align_bytes=64)
+                nc.vector.quantize_mx(codes[:].bitcast(FP8X4), plane[:], rounded[:])
+                w1_q[a, b, u] = (codes, plane)
+
+        picked = {}
+
+        def pick_page(i):
+            b, t = divmod(i, PACK)
+            nc.sync.dma_start(
+                pages[i][:], page0[PASS * b : PASS * (b + 1), :].rearrange("(p j) c -> p j c", j=PACK)[:, t, :]
+            )
+            old = ring.tile([P, S], F32, name="old", tag="old", bufs=4)
+            nc.vector.tensor_copy(old[:], pages[i][:].indirect(idx2[:]))
+            picked[i] = old
+
+        def update_page(i):
+            b, t = divmod(i, PACK)
+            gain = ring.tile([P, S], F32, name="gain", tag="gain", bufs=4)
+            for half in range(S // BANK):
+                cols = slice(BANK * half, BANK * (half + 1))
+                bank = psum.tile([P, BANK], F32, name="bank", tag="bank")
+                for a in range(K_PASSES):
+                    codes, plane = w1_q[a, b, t // 2]
+                    rows = slice(P * (t % 2), P * (t % 2 + 1))
+                    nc.tensor.matmul_mx(
+                        bank[:],
+                        lhsT=codes[:, rows].bitcast(FP8X4),
+                        lhsT_scale=plane[:, rows],
+                        rhs=v_codes[a][:, cols].bitcast(FP8X4),
+                        rhs_scale=v_planes[4 * a :, cols],
+                        start=(a == 0),
+                        stop=(a == K_PASSES - 1),
+                    )
+                nc.scalar.activation(gain[:, cols], bank[:], TANH, bias=b1_cols[:, b, t : t + 1])
+            nc.scalar.activation(gain[:], gain[:], COPY, bias=1.0, scale=0.5)
+            nc.vector.tensor_tensor(pages[i][:].indirect(idx2[:]), picked[i][:], gain[:], MULT)
+
+        gather_table(0)
+        for q in range(4):
+            nc.sync.dma_start(
+                tab_planes[32 * q : 32 * q + 4 * K_PASSES, :].bitcast(I32),
+                tab_scales[:, 4 * q : 4 * q + 4, :].bitcast(I32),
+            )
+        nc.vector.tensor_copy(v_planes[:], tab_planes[:].indirect(idx[:]))
+        quantize_w1(0, 0)
+        gather_table(1)
+        quantize_w1(1, 0)
+        nc.sync.dma_start(idx2[:], offs2)
+        gather_table(2)
+        nc.sync.dma_start(b1_cols[:], b1.rearrange("(b p t) -> p b t", p=P, t=PACK))
+        quantize_w1(2, 0)
+        for i in range(4):
+            pick_page(i)
+        for i in range(2):
+            update_page(i)
+            pick_page(4 + i)
+        for a in range(K_PASSES):
+            quantize_w1(a, 1)
+        for i in range(2, 4):
+            update_page(i)
+            pick_page(4 + i)
+
+        nc.sync.dma_start(idx3[:], offs3)
+        nc.sync.dma_start(w4_codes[:].bitcast(I32), w4_words.rearrange("a p c -> p a c").bitcast(I32))
+        for q in range(4):
+            nc.sync.dma_start(
+                w4_planes[32 * q : 32 * q + 4, :, :].bitcast(I32),
+                w4_scales[:, 4 * q : 4 * q + 4, :].rearrange("a r n -> r a n").bitcast(I32),
+            )
+        with nc.allow_non_contiguous_dma(reason="one factor a partition"):
+            nc.sync.dma_start(d_cols[:], d.rearrange("(n p) -> p n", p=P))
+
+        forecast = []
+        for c in range(M // FC_WIDTH):
+            tile = stage([P, R_PASSES * PACK, FC_WIDTH], F32, "fc%d" % c)
+            for b in range(R_PASSES):
+                nc.sync.dma_start(
+                    tile[:, PACK * b : PACK * (b + 1), :],
+                    fc[PASS * b : PASS * (b + 1), FC_WIDTH * c : FC_WIDTH * (c + 1)].rearrange(
+                        "(p j) c -> p j c", j=PACK
+                    ),
+                )
+            forecast.append(tile)
+
+        for i in range(4, 8):
+            update_page(i)
+
+        out_rows = out.rearrange("(n p) m -> p n m", p=P)
+        m0 = 0
+        for width in CHUNKS:
+            last = m0 + width == M
+            fc_tile = forecast[m0 // FC_WIDTH]
+            f0 = m0 % FC_WIDTH
+            x_q = []
+            for b in range(R_PASSES):
+                x = ring.tile([P, PACK, width], F32, name="x", tag="x", bufs=4)
+                for t in range(PACK):
+                    i = PACK * b + t
+                    nc.vector.tensor_tensor(
+                        x[:, t, :],
+                        pages[i][:].indirect(idx3[:, m0 // 16 : (m0 + width) // 16]),
+                        fc_tile[:, i, f0 : f0 + width],
+                        ADD,
+                    )
+                rounded = ring.tile([P, width * PACK], BF16, name="xbf", tag="xbf", bufs=4, align_bytes=64)
+                nc.scalar.copy(
+                    rounded[:].rearrange("p (c e t) -> p c t e", e=4, t=PACK),
+                    x[:].rearrange("p t (c e) -> p c t e", e=4),
+                )
+                codes = ring.tile([P, width], U32, name="xc", tag="xc", bufs=4, align_bytes=64)
+                plane = ring.tile([P, width], U8, name="xs", tag="xs", bufs=4, align_bytes=64)
+                nc.vector.quantize_mx(codes[:].bitcast(FP8X4), plane[:], rounded[:])
+                x_q.append((codes, plane))
+            per_bank = 2 if width == 256 else 3
+            for n0 in range(0, N_TILES, per_bank):
+                bank = psum.tile([P, BANK], F32, name="bank", tag="bank")
+                for b in range(R_PASSES):
+                    codes, plane = x_q[b]
+                    for k in range(per_bank):
+                        n = n0 + k
+                        nc.tensor.matmul_mx(
+                            bank[:, width * k : width * (k + 1)],
+                            lhsT=w4_codes[:, b, 2 * P * n : 2 * P * (n + 1)].bitcast(FP4X4),
+                            lhsT_scale=w4_planes[:, b, P * n : P * (n + 1)],
+                            rhs=codes[:].bitcast(FP8X4),
+                            rhs_scale=plane[:],
+                            start=(b == 0 and k == 0),
+                            stop=(b == R_PASSES - 1 and k == per_bank - 1),
+                        )
+                y = ring.tile([P, per_bank, width], F32, name="y", tag="y", bufs=4)
+                for k in range(per_bank):
+                    n = n0 + k
+                    sums = bank[:, width * k : width * (k + 1)]
+                    if last and n0 > 0:
+                        nc.vector.tensor_scalar(y[:, k, :], sums, d_cols[:, n : n + 1], None, MULT)
+                    else:
+                        nc.scalar.activation(y[:, k, :], sums, COPY, scale=d_cols[:, n : n + 1])
+                nc.sync.dma_start(out_rows[:, n0 : n0 + per_bank, m0 : m0 + width], y[:])
+            m0 = m0 + width

@@ -71,16 +71,16 @@ def tile_list_heater_point_trust_kernel(
                 raw[:],
                 w1[PASS * a : PASS * (a + 1), PASS * b : PASS * (b + 1)].rearrange("(p j) c -> p j c", j=PACK),
             )
+            rounded = ring.tile([P, PACK * PASS], BF16, name="w1bf", tag="w1bf", bufs=3, align_bytes=64)
             for u in range(2):
-                rounded = ring.tile([P, 2 * PASS], BF16, name="w1bf", tag="w1bf", bufs=4, align_bytes=64)
                 nc.scalar.copy(
-                    rounded[:].rearrange("p (e m j) -> p m j e", e=2, j=PACK),
+                    rounded[:].rearrange("p (u e m j) -> p u m j e", u=2, e=2, j=PACK)[:, u],
                     raw[:].rearrange("p j (m u e) -> p u m j e", u=2, e=2)[:, u],
                 )
-                codes = keep.tile([P, 2 * P], U32, name="w1c%d%d%d" % (a, b, u), align_bytes=64)
-                plane = keep.tile([P, 2 * P], U8, name="w1s%d%d%d" % (a, b, u), align_bytes=64)
-                nc.vector.quantize_mx(codes[:].bitcast(FP8X4), plane[:], rounded[:])
-                w1_q[a, b, u] = (codes, plane)
+            codes = keep.tile([P, PASS], U32, name="w1c%d%d" % (a, b), align_bytes=64)
+            plane = keep.tile([P, PASS], U8, name="w1s%d%d" % (a, b), align_bytes=64)
+            nc.vector.quantize_mx(codes[:].bitcast(FP8X4), plane[:], rounded[:])
+            w1_q[a, b] = (codes, plane)
 
         picked = {}
 
@@ -100,8 +100,8 @@ def tile_list_heater_point_trust_kernel(
                 cols = slice(BANK * half, BANK * (half + 1))
                 bank = psum.tile([P, BANK], F32, name="bank", tag="bank")
                 for a in range(K_PASSES):
-                    codes, plane = w1_q[a, b, t // 2]
-                    rows = slice(P * (t % 2), P * (t % 2 + 1))
+                    codes, plane = w1_q[a, b]
+                    rows = slice(P * t, P * (t + 1))
                     nc.tensor.matmul_mx(
                         bank[:],
                         lhsT=codes[:, rows].bitcast(FP8X4),
@@ -129,13 +129,14 @@ def tile_list_heater_point_trust_kernel(
         gather_table(2)
         nc.sync.dma_start(b1_cols[:], b1.rearrange("(b p t) -> p b t", p=P, t=PACK))
         quantize_w1(2, 0)
-        for i in range(4):
+        for i in range(3):
             pick_page(i)
         for i in range(2):
             update_page(i)
-            pick_page(4 + i)
         for a in range(K_PASSES):
             quantize_w1(a, 1)
+        for i in range(3, 6):
+            pick_page(i)
         for i in range(2, 4):
             update_page(i)
             pick_page(4 + i)

@@ -26,7 +26,6 @@ K_PASSES = K // PASS
 R_PASSES = H // PASS
 N_TILES = N // P
 FC_WIDTH = 256
-CHUNKS = (256, 256, 256, 128, 128)
 
 
 def tile_list_heater_point_trust_kernel(
@@ -65,7 +64,7 @@ def tile_list_heater_point_trust_kernel(
 
         w1_q = {}
 
-        def quantize_w1(a, b):
+        def quantize_w1(a, b, pieces):
             raw = stage([P, PACK, PASS], F32, "w1raw%d%d" % (a, b))
             nc.sync.dma_start(
                 raw[:],
@@ -79,7 +78,13 @@ def tile_list_heater_point_trust_kernel(
                 )
             codes = keep.tile([P, PASS], U32, name="w1c%d%d" % (a, b), align_bytes=64)
             plane = keep.tile([P, PASS], U8, name="w1s%d%d" % (a, b), align_bytes=64)
-            nc.vector.quantize_mx(codes[:].bitcast(FP8X4), plane[:], rounded[:])
+            step = PASS // pieces
+            for c0 in range(0, PASS, step):
+                nc.vector.quantize_mx(
+                    codes[:, c0 : c0 + step].bitcast(FP8X4),
+                    plane[:, c0 : c0 + step],
+                    rounded[:, PACK * c0 : PACK * (c0 + step)],
+                )
             w1_q[a, b] = (codes, plane)
 
         picked = {}
@@ -116,25 +121,26 @@ def tile_list_heater_point_trust_kernel(
             nc.vector.tensor_tensor(pages[i][:].indirect(idx2[:]), picked[i][:], gain[:], MULT)
 
         gather_table(0)
+        quantize_w1(0, 0, 1)
         for q in range(4):
             nc.sync.dma_start(
                 tab_planes[32 * q : 32 * q + 4 * K_PASSES, :].bitcast(I32),
                 tab_scales[:, 4 * q : 4 * q + 4, :].bitcast(I32),
             )
         nc.vector.tensor_copy(v_planes[:], tab_planes[:].indirect(idx[:]))
-        quantize_w1(0, 0)
         gather_table(1)
-        quantize_w1(1, 0)
+        quantize_w1(1, 0, 1)
         nc.sync.dma_start(idx2[:], offs2)
         gather_table(2)
         nc.sync.dma_start(b1_cols[:], b1.rearrange("(b p t) -> p b t", p=P, t=PACK))
-        quantize_w1(2, 0)
-        for i in range(3):
+        pick_page(0)
+        quantize_w1(2, 0, 2)
+        for i in range(1, 3):
             pick_page(i)
         for i in range(2):
             update_page(i)
         for a in range(K_PASSES):
-            quantize_w1(a, 1)
+            quantize_w1(a, 1, 1)
         for i in range(3, 6):
             pick_page(i)
         for i in range(2, 4):
@@ -167,54 +173,73 @@ def tile_list_heater_point_trust_kernel(
             update_page(i)
 
         out_rows = out.rearrange("(n p) m -> p n m", p=P)
-        m0 = 0
-        for width in CHUNKS:
-            last = m0 + width == M
+        x_q = {}
+
+        def quantize_x(b, m0, width, round_on_vector):
             fc_tile = forecast[m0 // FC_WIDTH]
             f0 = m0 % FC_WIDTH
-            x_q = []
-            for b in range(R_PASSES):
-                x = ring.tile([P, PACK, width], F32, name="x", tag="x", bufs=4)
-                for t in range(PACK):
-                    i = PACK * b + t
-                    nc.vector.tensor_tensor(
-                        x[:, t, :],
-                        pages[i][:].indirect(idx3[:, m0 // 16 : (m0 + width) // 16]),
-                        fc_tile[:, i, f0 : f0 + width],
-                        ADD,
-                    )
-                rounded = ring.tile([P, width * PACK], BF16, name="xbf", tag="xbf", bufs=4, align_bytes=64)
-                nc.scalar.copy(
-                    rounded[:].rearrange("p (c e t) -> p c t e", e=4, t=PACK),
-                    x[:].rearrange("p t (c e) -> p c t e", e=4),
+            x = ring.tile([P, PACK, width], F32, name="x", tag="x", bufs=2)
+            for t in range(PACK):
+                i = PACK * b + t
+                nc.vector.tensor_tensor(
+                    x[:, t, :],
+                    pages[i][:].indirect(idx3[:, m0 // 16 : (m0 + width) // 16]),
+                    fc_tile[:, i, f0 : f0 + width],
+                    ADD,
                 )
-                codes = ring.tile([P, width], U32, name="xc", tag="xc", bufs=4, align_bytes=64)
-                plane = ring.tile([P, width], U8, name="xs", tag="xs", bufs=4, align_bytes=64)
-                nc.vector.quantize_mx(codes[:].bitcast(FP8X4), plane[:], rounded[:])
-                x_q.append((codes, plane))
-            per_bank = 2 if width == 256 else 3
+            rounded = ring.tile([P, width * PACK], BF16, name="xbf", tag="xbf", bufs=2, align_bytes=64)
+            copy = nc.vector.tensor_copy if round_on_vector else nc.scalar.copy
+            copy(
+                rounded[:].rearrange("p (c e t) -> p c t e", e=4, t=PACK),
+                x[:].rearrange("p t (c e) -> p c t e", e=4),
+            )
+            codes = ring.tile([P, width], U32, name="xc", tag="xc", bufs=4, align_bytes=64)
+            plane = ring.tile([P, width], U8, name="xs", tag="xs", bufs=4, align_bytes=64)
+            nc.vector.quantize_mx(codes[:].bitcast(FP8X4), plane[:], rounded[:])
+            for m in range(0, width, P):
+                x_q[b, m0 + m] = (codes, plane, m)
+
+        def multiply_x(m0, width):
+            per_bank = 2 if width == FC_WIDTH else 3
             for n0 in range(0, N_TILES, per_bank):
                 bank = psum.tile([P, BANK], F32, name="bank", tag="bank")
                 for b in range(R_PASSES):
-                    codes, plane = x_q[b]
+                    codes, plane, first = x_q[b, m0]
                     for k in range(per_bank):
                         n = n0 + k
                         nc.tensor.matmul_mx(
                             bank[:, width * k : width * (k + 1)],
                             lhsT=w4_codes[:, b, 2 * P * n : 2 * P * (n + 1)].bitcast(FP4X4),
                             lhsT_scale=w4_planes[:, b, P * n : P * (n + 1)],
-                            rhs=codes[:].bitcast(FP8X4),
-                            rhs_scale=plane[:],
+                            rhs=codes[:, first : first + width].bitcast(FP8X4),
+                            rhs_scale=plane[:, first : first + width],
                             start=(b == 0 and k == 0),
                             stop=(b == R_PASSES - 1 and k == per_bank - 1),
                         )
-                y = ring.tile([P, per_bank, width], F32, name="y", tag="y", bufs=4)
-                for k in range(per_bank):
-                    n = n0 + k
-                    sums = bank[:, width * k : width * (k + 1)]
-                    if last and n0 > 0:
-                        nc.vector.tensor_scalar(y[:, k, :], sums, d_cols[:, n : n + 1], None, MULT)
-                    else:
+                y = ring.tile([P, per_bank, width], F32, name="y", tag="y", bufs=7)
+                if width < FC_WIDTH and n0 > 0:
+                    nc.vector.tensor_tensor(
+                        y[:],
+                        bank[:, : per_bank * width].rearrange("p (k m) -> p k m", k=per_bank),
+                        d_cols[:, n0 : n0 + per_bank].unsqueeze(2).to_broadcast([P, per_bank, width]),
+                        MULT,
+                    )
+                else:
+                    for k in range(per_bank):
+                        n = n0 + k
+                        sums = bank[:, width * k : width * (k + 1)]
                         nc.scalar.activation(y[:, k, :], sums, COPY, scale=d_cols[:, n : n + 1])
                 nc.sync.dma_start(out_rows[:, n0 : n0 + per_bank, m0 : m0 + width], y[:])
-            m0 = m0 + width
+
+        last = M - FC_WIDTH
+        for m0 in range(0, last, FC_WIDTH):
+            for b in range(R_PASSES):
+                quantize_x(b, m0, FC_WIDTH, False)
+            if m0 > 0:
+                multiply_x(m0 - FC_WIDTH, FC_WIDTH)
+        quantize_x(0, last, FC_WIDTH, False)
+        quantize_x(1, last, P, False)
+        multiply_x(last - FC_WIDTH, FC_WIDTH)
+        quantize_x(1, last + P, P, True)
+        multiply_x(last, P)
+        multiply_x(last + P, P)

@@ -26,6 +26,7 @@ K_PASSES = K // PASS
 R_PASSES = H // PASS
 N_TILES = N // P
 FC_WIDTH = 256
+EARLY_PAGES = 3
 
 
 def tile_list_heater_point_trust_kernel(
@@ -94,9 +95,10 @@ def tile_list_heater_point_trust_kernel(
             nc.sync.dma_start(
                 pages[i][:], page0[PASS * b : PASS * (b + 1), :].rearrange("(p j) c -> p j c", j=PACK)[:, t, :]
             )
-            old = ring.tile([P, S], F32, name="old", tag="old", bufs=4)
-            nc.vector.tensor_copy(old[:], pages[i][:].indirect(idx2[:]))
-            picked[i] = old
+            if i < EARLY_PAGES:
+                old = ring.tile([P, S], F32, name="old", tag="old", bufs=4)
+                nc.vector.tensor_copy(old[:], pages[i][:].indirect(idx2[:]))
+                picked[i] = old
 
         def update_page(i):
             b, t = divmod(i, PACK)
@@ -118,7 +120,12 @@ def tile_list_heater_point_trust_kernel(
                     )
                 nc.scalar.activation(gain[:, cols], bank[:], TANH, bias=b1_cols[:, b, t : t + 1])
             nc.scalar.activation(gain[:], gain[:], COPY, bias=1.0, scale=0.5)
-            nc.vector.tensor_tensor(pages[i][:].indirect(idx2[:]), picked[i][:], gain[:], MULT)
+            if i < EARLY_PAGES:
+                nc.vector.tensor_tensor(pages[i][:].indirect(idx2[:]), picked[i][:], gain[:], MULT)
+            else:
+                new = ring.tile([P, S], F32, name="new", tag="old", bufs=4)
+                nc.vector.tensor_tensor(new[:], pages[i][:].indirect(idx2[:]), gain[:], MULT)
+                nc.vector.tensor_copy(pages[i][:].indirect(idx2[:]), new[:])
 
         gather_table(0)
         quantize_w1(0, 0, 1)

from contextlib import ExitStack

import concourse.mybir as mybir

K, T, S, H, T2, M, N = 1536, 2048, 1024, 1024, 2048, 1024, 768
FLOPS = 2 * K * H * S + 2 * H * N * M

F32 = mybir.dt.float32
BF16 = mybir.dt.bfloat16
I32 = mybir.dt.int32
U32 = mybir.dt.uint32
U16 = mybir.dt.uint16
U8 = mybir.dt.uint8
FP8X4 = mybir.dt.float8_e4m3fn_x4
FP4X4 = mybir.dt.float4_e2m1fn_x4
MULT = mybir.AluOpType.mult
ADD = mybir.AluOpType.add
COPY = mybir.ActivationFunctionType.Copy
TANH = mybir.ActivationFunctionType.Tanh

P = 128
PACK = 4
PASS = P * PACK
BANK = 512
K_PASSES = K // PASS
R_PASSES = H // PASS
N_TILES = N // P
FC_WIDTH = 256
EARLY_PAGES = 3


def tile_list_heater_point_trust_kernel(
    tc, tab_words, tab_scales, offs, offs2, offs3, w1, b1, page0, fc, w4_words, w4_scales, d, out
):
    nc = tc.nc
    with ExitStack() as ctx:
        keep = ctx.enter_context(tc.tile_pool(name="keep", bufs=1))
        ring = ctx.enter_context(tc.tile_pool(name="ring", bufs=2))
        psum = ctx.enter_context(tc.psum_pool(name="psum", bufs=8))

        def stage(shape, dtype, name):
            return ring.tile(shape, dtype, name=name, tag="stage", bufs=6)

        idx = keep.tile([P, S // 16], U16, name="idx")
        idx2 = keep.tile([P, S // 16], U16, name="idx2")
        idx3 = keep.tile([P, M // 16], U16, name="idx3")
        tab_planes = keep.tile([P, T], U8, name="tab_planes")
        w4_planes = keep.tile([P, R_PASSES, N], U8, name="w4_planes", align_bytes=64)
        w4_codes = keep.tile([P, R_PASSES, 2 * N], U8, name="w4_codes", align_bytes=64)
        b1_cols = keep.tile([P, R_PASSES, PACK], F32, name="b1_cols")
        d_cols = keep.tile([P, N_TILES], F32, name="d_cols")
        v_planes = keep.tile([P, S], U8, name="v_planes", align_bytes=64)
        v_codes = [keep.tile([P, S], U32, name="v_codes%d" % a, align_bytes=64) for a in range(K_PASSES)]
        pages = [keep.tile([P, T2], F32, name="page%d" % i) for i in range(R_PASSES * PACK)]

        nc.vector.memset(tab_planes[:].bitcast(I32), 0)
        nc.vector.memset(w4_planes[:].rearrange("p a n -> p (a n)").bitcast(I32), 0)

        nc.sync.dma_start(idx[:], offs)

        def gather_table(a):
            words = stage([P, T], I32, "words%d" % a)
            nc.sync.dma_start(words[:], tab_words[a].rearrange("p n i -> p (n i)").bitcast(I32))
            nc.vector.tensor_copy(v_codes[a][:], words[:].bitcast(U32).indirect(idx[:]))

        w1_q = {}

        def quantize_w1(a, b, pieces):
            raw = stage([P, PACK, PASS], F32, "w1raw%d%d" % (a, b))
            nc.sync.dma_start(
                raw[:],
                w1[PASS * a : PASS * (a + 1), PASS * b : PASS * (b + 1)].rearrange("(p j) c -> p j c", j=PACK),
            )
            rounded = ring.tile([P, PACK * PASS], BF16, name="w1bf", tag="w1bf", bufs=3, align_bytes=64)
            for u in range(2):
                nc.scalar.copy(
                    rounded[:].rearrange("p (u e m j) -> p u m j e", u=2, e=2, j=PACK)[:, u],
                    raw[:].rearrange("p j (m u e) -> p u m j e", u=2, e=2)[:, u],
                )
            codes = keep.tile([P, PASS], U32, name="w1c%d%d" % (a, b), align_bytes=64)
            plane = keep.tile([P, PASS], U8, name="w1s%d%d" % (a, b), align_bytes=64)
            step = PASS // pieces
            for c0 in range(0, PASS, step):
                nc.vector.quantize_mx(
                    codes[:, c0 : c0 + step].bitcast(FP8X4),
                    plane[:, c0 : c0 + step],
                    rounded[:, PACK * c0 : PACK * (c0 + step)],
                )
            w1_q[a, b] = (codes, plane)

        picked = {}

        def pick_page(i):
            b, t = divmod(i, PACK)
            nc.sync.dma_start(
                pages[i][:], page0[PASS * b : PASS * (b + 1), :].rearrange("(p j) c -> p j c", j=PACK)[:, t, :]
            )
            if i < EARLY_PAGES:
                old = ring.tile([P, S], F32, name="old", tag="old", bufs=4)
                nc.vector.tensor_copy(old[:], pages[i][:].indirect(idx2[:]))
                picked[i] = old

        def update_page(i):
            b, t = divmod(i, PACK)
            gain = ring.tile([P, S], F32, name="gain", tag="gain", bufs=4)
            for half in range(S // BANK):
                cols = slice(BANK * half, BANK * (half + 1))
                bank = psum.tile([P, BANK], F32, name="bank", tag="bank")
                for a in range(K_PASSES):
                    codes, plane = w1_q[a, b]
                    rows = slice(P * t, P * (t + 1))
                    nc.tensor.matmul_mx(
                        bank[:],
                        lhsT=codes[:, rows].bitcast(FP8X4),
                        lhsT_scale=plane[:, rows],
                        rhs=v_codes[a][:, cols].bitcast(FP8X4),
                        rhs_scale=v_planes[4 * a :, cols],
                        start=(a == 0),
                        stop=(a == K_PASSES - 1),
                    )
                nc.scalar.activation(gain[:, cols], bank[:], TANH, bias=b1_cols[:, b, t : t + 1])
            nc.scalar.activation(gain[:], gain[:], COPY, bias=1.0, scale=0.5)
            if i < EARLY_PAGES:
                nc.vector.tensor_tensor(pages[i][:].indirect(idx2[:]), picked[i][:], gain[:], MULT)
            else:
                new = ring.tile([P, S], F32, name="new", tag="old", bufs=4)
                nc.vector.tensor_tensor(new[:], pages[i][:].indirect(idx2[:]), gain[:], MULT)
                nc.vector.tensor_copy(pages[i][:].indirect(idx2[:]), new[:])

        gather_table(0)
        quantize_w1(0, 0, 1)
        for q in range(4):
            nc.sync.dma_start(
                tab_planes[32 * q : 32 * q + 4 * K_PASSES, :].bitcast(I32),
                tab_scales[:, 4 * q : 4 * q + 4, :].bitcast(I32),
            )
        nc.vector.tensor_copy(v_planes[:], tab_planes[:].indirect(idx[:]))
        gather_table(1)
        quantize_w1(1, 0, 1)
        nc.sync.dma_start(idx2[:], offs2)
        gather_table(2)
        nc.sync.dma_start(b1_cols[:], b1.rearrange("(b p t) -> p b t", p=P, t=PACK))
        pick_page(0)
        quantize_w1(2, 0, 2)
        for i in range(1, 3):
            pick_page(i)
        for i in range(2):
            update_page(i)
        for a in range(K_PASSES):
            quantize_w1(a, 1, 1)
        for i in range(3, 6):
            pick_page(i)
        for i in range(2, 4):
            update_page(i)
            pick_page(4 + i)

        nc.sync.dma_start(idx3[:], offs3)
        nc.sync.dma_start(w4_codes[:].bitcast(I32), w4_words.rearrange("a p c -> p a c").bitcast(I32))
        for q in range(4):
            nc.sync.dma_start(
                w4_planes[32 * q : 32 * q + 4, :, :].bitcast(I32),
                w4_scales[:, 4 * q : 4 * q + 4, :].rearrange("a r n -> r a n").bitcast(I32),
            )
        with nc.allow_non_contiguous_dma(reason="one factor a partition"):
            nc.sync.dma_start(d_cols[:], d.rearrange("(n p) -> p n", p=P))

        forecast = []
        for c in range(M // FC_WIDTH):
            tile = stage([P, R_PASSES * PACK, FC_WIDTH], F32, "fc%d" % c)
            for b in range(R_PASSES):
                nc.sync.dma_start(
                    tile[:, PACK * b : PACK * (b + 1), :],
                    fc[PASS * b : PASS * (b + 1), FC_WIDTH * c : FC_WIDTH * (c + 1)].rearrange(
                        "(p j) c -> p j c", j=PACK
                    ),
                )
            forecast.append(tile)

        for i in range(4, 8):
            update_page(i)

        out_rows = out.rearrange("(n p) m -> p n m", p=P)
        x_q = {}

        def quantize_x(b, m0, width, round_on_vector):
            fc_tile = forecast[m0 // FC_WIDTH]
            f0 = m0 % FC_WIDTH
            x = ring.tile([P, PACK, width], F32, name="x", tag="x", bufs=2)
            for t in range(PACK):
                i = PACK * b + t
                nc.vector.tensor_tensor(
                    x[:, t, :],
                    pages[i][:].indirect(idx3[:, m0 // 16 : (m0 + width) // 16]),
                    fc_tile[:, i, f0 : f0 + width],
                    ADD,
                )
            rounded = ring.tile([P, width * PACK], BF16, name="xbf", tag="xbf", bufs=2, align_bytes=64)
            copy = nc.vector.tensor_copy if round_on_vector else nc.scalar.copy
            copy(
                rounded[:].rearrange("p (c e t) -> p c t e", e=4, t=PACK),
                x[:].rearrange("p t (c e) -> p c t e", e=4),
            )
            codes = ring.tile([P, width], U32, name="xc", tag="xc", bufs=4, align_bytes=64)
            plane = ring.tile([P, width], U8, name="xs", tag="xs", bufs=4, align_bytes=64)
            nc.vector.quantize_mx(codes[:].bitcast(FP8X4), plane[:], rounded[:])
            for m in range(0, width, P):
                x_q[b, m0 + m] = (codes, plane, m)

        def multiply_x(m0, width):
            per_bank = 2 if width == FC_WIDTH else 3
            for n0 in range(0, N_TILES, per_bank):
                bank = psum.tile([P, BANK], F32, name="bank", tag="bank")
                for b in range(R_PASSES):
                    codes, plane, first = x_q[b, m0]
                    for k in range(per_bank):
                        n = n0 + k
                        nc.tensor.matmul_mx(
                            bank[:, width * k : width * (k + 1)],
                            lhsT=w4_codes[:, b, 2 * P * n : 2 * P * (n + 1)].bitcast(FP4X4),
                            lhsT_scale=w4_planes[:, b, P * n : P * (n + 1)],
                            rhs=codes[:, first : first + width].bitcast(FP8X4),
                            rhs_scale=plane[:, first : first + width],
                            start=(b == 0 and k == 0),
                            stop=(b == R_PASSES - 1 and k == per_bank - 1),
                        )
                y = ring.tile([P, per_bank, width], F32, name="y", tag="y", bufs=7)
                if width < FC_WIDTH and n0 > 0:
                    nc.vector.tensor_tensor(
                        y[:],
                        bank[:, : per_bank * width].rearrange("p (k m) -> p k m", k=per_bank),
                        d_cols[:, n0 : n0 + per_bank].unsqueeze(2).to_broadcast([P, per_bank, width]),
                        MULT,
                    )
                else:
                    for k in range(per_bank):
                        n = n0 + k
                        sums = bank[:, width * k : width * (k + 1)]
                        nc.scalar.activation(y[:, k, :], sums, COPY, scale=d_cols[:, n : n + 1])
                nc.sync.dma_start(out_rows[:, n0 : n0 + per_bank, m0 : m0 + width], y[:])

        last = M - FC_WIDTH
        for m0 in range(0, last, FC_WIDTH):
            for b in range(R_PASSES):
                quantize_x(b, m0, FC_WIDTH, False)
            if m0 > 0:
                multiply_x(m0 - FC_WIDTH, FC_WIDTH)
        quantize_x(0, last, FC_WIDTH, False)
        quantize_x(1, last, P, False)
        multiply_x(last - FC_WIDTH, FC_WIDTH)
        quantize_x(1, last + P, P, True)
        multiply_x(last, P)
        multiply_x(last + P, P)
